import numpy as np, ml_dtypes
CORES = [66,74,82,90,194,202,210,218]
N = 8
BF = ml_dtypes.bfloat16
def gentries(a):
    return np.ascontiguousarray(a.reshape(8, 16, -1).transpose(0, 2, 1)).reshape(8, -1)
def gtable(e):
    e = np.asarray(e); return np.ascontiguousarray(e.reshape(8, -1, 16).transpose(0, 2, 1)).reshape(128, -1).astype(np.int32)
K, D, SH = 256, 4096, 2
def sized(rng):
    return rng.standard_normal((N, 128, D), dtype=np.float32) * np.exp2(rng.integers(-1, 2, (N, 128, 1))).astype(np.float32)
def hashes(a, b):
    return np.repeat(np.stack([a, b], 2), 16, axis=1).astype(np.int32)
def lists(e):
    return np.stack([gtable(u) for u in e])
def setup_inputs(rng):
    a = np.stack([rng.permutation(255)[:8] + 1 for r in range(N)]); b = rng.integers(0, 65536, (N, 8))
    return {"mat": sized(rng).astype(BF), "ids": lists(rng.integers(0, 65536, (N, 8, K))), "hs": hashes(a, b)}
def setup_inputs_ends(rng):
    e = rng.integers(0, 65536, (N, 8, K)); e = np.where(rng.random(e.shape) < 0.5, rng.choice(np.array([0, 1, 65534, 65535]), e.shape), e)
    e[:, :, 0] = 0; e[:, :, 1] = 1 << SH; e[:, :, -1] = 65535
    top = (D - 1) << SH; low = (1 << SH) - 1
    a = rng.choice(np.array([0, 1, 254, 255]), (N, 8)); b = rng.choice(np.array([0, 1, low, top, top + low, 65535]), (N, 8))
    for r in range(N):
        a[r, r % 8], b[r, r % 8] = 1, top
        a[r, (r + 1) % 8], b[r, (r + 1) % 8] = 255, 65535
        a[r, (r + 2) % 8] = 0
        a[r, (r + 3) % 8], b[r, (r + 3) % 8] = 1, top + low
    return {"mat": sized(rng).astype(BF), "ids": lists(e), "hs": hashes(a, b)}
def setup_inputs_one(rng):
    d = setup_inputs(rng); e = rng.integers(0, 65536, (N, 8, K)); o = rng.permutation(N)
    e[o[0]] = rng.permutation(65536)[:8, None]; e[o[1]] = e[o[2]]; e[o[3]] = np.repeat(e[o[3], :, :K // 16], 16, axis=1)
    d["ids"] = lists(e); d["hs"][rng.integers(0, N), :, 0] = 0; return d
def setup_inputs_turns(rng):
    d = setup_inputs(rng); p = np.argsort(rng.random((N, 8, D, 4)), axis=3)
    w = (rng.integers(128, 256, p.shape) * (2 * rng.integers(0, 2, p.shape) - 1)).astype(np.float32) * np.float32(2.0 ** -7)
    m = np.where(p[..., None] == np.arange(4), w[..., None], np.float32(0))
    d["mat"] = np.ascontiguousarray(m.transpose(0, 1, 3, 4, 2)).reshape(N, 128, D).astype(BF); return d
def setup_inputs_spread(rng):
    d = setup_inputs(rng); k = (N, 8, 1, D)
    z = (np.exp2(rng.integers(-2, 3, k)) * (rng.random(k) > 0.03125)).astype(np.float32)
    d["mat"] = (sized(rng).reshape(N, 8, 16, D) * z).reshape(N, 128, D).astype(BF); return d
def check_inputs(d):
    bad = []; h = d["hs"].reshape(N, 8, 16, 2)
    if not (np.abs(d["mat"].astype(np.float32)) <= 8192).all(): bad.append("size of mat")
    if not ((d["ids"] >= 0) & (d["ids"] <= 65535)).all(): bad.append("range of ids")
    if not ((h >= 0) & (h <= np.array([255, 65535]))).all(): bad.append("range of hs")
    if not (h == h[:, :, :1]).all(): bad.append("rows of hs alike in a group")
    return bad
def reference(mat, ids, hs):
    y = np.zeros((N, 32, K), np.float64); m = mat.astype(np.float64).reshape(N, 8, 16, D); h = hs.astype(np.int64)[:, ::16]
    for r in range(N):
        i = gentries(ids[r]).astype(np.int64)
        v = np.zeros((8, 4, K), np.float64); v[:, 0] = 1
        for q in range(N):
            t = ((i * h[q, :, :1] + h[q, :, 1:]) >> SH) & (D - 1)
            x = np.take_along_axis(m[q], t[:, None, :], 2).reshape(8, 4, 4, K)
            v = np.sum(v[:, :, None, :] * x, axis=1)
        y[r] = v.reshape(32, K)
    return {"y": y.astype(np.float32)}

@@ -1,0 +1,181 @@
+from concourse.bass import DstId, RemoteDMATransfer
+from concourse.mybir import AluOpType, ActivationFunctionType
+
+K, D = 256, 4096
+L = K // 16
+H = K // 2
+GROUPS = [(1, 2), (3, 4), (5, 6, 7)]
+
+SCRATCH = {
+    "idd": ("dram", [128, L], "int32"),
+    "idl": ("sbuf", [128, 8 * L], "int32"),
+    "hsi": ("sbuf", [128, 2], "int32"),
+    "hsf": ("sbuf", [128, 2], "float32"),
+    "t1": ("sbuf", [128, 8 * L], "int32"),
+    "t2": ("sbuf", [128, 8 * L], "int32"),
+    "off": ("sbuf", [128, 8 * L], "uint16"),
+    "tab": ("sbuf", [128, D], "bfloat16"),
+    "pk": ("sbuf", [128, 8 * K], "bfloat16"),
+    "ld": ("sbuf", [128, 8 * K], "bfloat16"),
+    "s32": ("sbuf", [128, 32], "float32"),
+    "z32": ("sbuf", [128, 32], "float32"),
+    "sf": ("sbuf", [128, 128], "float32"),
+    "s0": ("sbuf", [128, 128], "bfloat16"),
+    "pra": ("sbuf", [128, H], "float32"),
+    "prb": ("sbuf", [128, H], "float32"),
+    "ysb": ("sbuf", [32, K], "float32"),
+    "psa": ("psum", [128, 512], "float32"),
+    "psb": ("psum", [128, 512], "float32"),
+}
+SEMAPHORES = (["ldd", "ldi", "ldh", "ldm", "sent", "h", "off_s", "sel", "ms", "exp", "va", "vb", "ta", "tb",
+               "ya", "yb", "sta", "stb", "g7b"]
+              + ["id%d" % i for i in range(len(GROUPS))]
+              + ["gk%d" % k for k in range(8)]
+              + ["pk_s%d" % q for q in range(8)])
+
+
+def bits(engines):
+    m = 0
+    for e in engines:
+        m |= 1 << e
+    return m
+
+
+def dst(topo, d, core):
+    rid, pid = topo.addr(d, core)
+    return DstId(rid=rid, pnc=pid)
+
+
+def rank_program(g, core, T, topo):
+    rank = T.rank_of(core)
+    if rank is None:
+        return
+    peer = [T.cores[rank ^ k] for k in range(8)]
+    S = T.sem
+    V, P, A = g.vector, g.tensor, g.scalar
+    copy = ActivationFunctionType.Copy
+
+    g.sync.dma_start(T.idd[:], T.ids[:]).then_inc(S.ldd, 16)
+    A.dma_start(T.idl[:, 0:L], T.ids[:]).then_inc(S.ldi, 16)
+    A.dma_start(T.hsi[:], T.hs[:]).then_inc(S.ldh, 16)
+    g.sync.dma_start(T.tab[:], T.mat[:]).then_inc(S.ldm, 16)
+
+    sent = 0
+    g.wait_ge(S.ldd, 16)
+    for i, ks in enumerate(GROUPS):
+        eng = topo.engines(core, peer[ks[0]])
+        g.remote_dma_fused([RemoteDMATransfer(
+            dst_ids=[dst(topo, peer[k], core) for k in ks], dma_engine_mask=bits(eng), remote_sem=S["id%d" % i],
+            srcs=[T.idd[:]], dsts=[T.idl[:, k * L:(k + 1) * L] for k in ks])], local_sem=S.sent)
+        sent += len(eng)
+    g.wait_ge(S.ms, 2)
+    g.affine_select(T.z32[:], T.z32[:], [[-16, 8], [-1, 4]], AluOpType.not_equal, 1.0, 0, 1).then_inc(S.sel, 1)
+    for a in range(4):
+        g.affine_select(T.s32[:], T.s32[:], [[-16, 8], [-1, 4]], AluOpType.not_equal, 1.0, -4 * a, 1).then_inc(S.sel, 1)
+        g.wait_ge(S.sel, a + 2)
+    for ks in [(1, 2), (3, 4), (5, 6), (7,)]:
+        for k in ks:
+            g.wait_ge(S["gk%d" % k], 1)
+            if k == 7:
+                g.wait_ge(S.g7b, 1)
+        tr = []
+        for i, k in enumerate(ks):
+            eng = topo.engines(core, peer[k])
+            n = len(eng) // len(ks)
+            eng = eng[i * n:(i + 1) * n]
+            tr.append(RemoteDMATransfer(
+                dst_ids=[dst(topo, peer[k], core)], dma_engine_mask=bits(eng), remote_sem=S["pk_s%d" % rank],
+                srcs=[T.pk[:, k * K:(k + 1) * K]], dsts=[T.ld[:, rank * K:(rank + 1) * K]]))
+            sent += n
+        g.remote_dma_fused(tr, local_sem=S.sent)
+    g.wait_ge(S.sent, sent)
+
+    h = [0]
+
+    def hashes(k0, k1, n):
+        c = slice(k0 * L, k1 * L)
+        V.tensor_scalar(T.t1[:, c], T.idl[:, c], T.hsf[:, 0:1], T.hsf[:, 1:2], AluOpType.mult, AluOpType.add).then_inc(S.h, 1)
+        h[0] += 1
+        V.wait_ge(S.h, h[0])
+        V.tensor_scalar(T.t2[:, c], T.t1[:, c], 2, D - 1, AluOpType.logical_shift_right, AluOpType.bitwise_and).then_inc(S.h, 1)
+        h[0] += 1
+        V.wait_ge(S.h, h[0])
+        V.tensor_copy(T.off[:, c], T.t2[:, c]).then_inc(S.off_s, 1)
+        V.wait_ge(S.off_s, n)
+
+    def win(o0, o1):
+        return T.tab[:, 0:D].indirect(T.off[:, o0:o1])
+
+    def gather_v(o0, o1, sem):
+        V.tensor_copy(T.pk[:, 16 * o0:16 * o1], win(o0, o1)).then_inc(sem, 1)
+
+    def gather_a(o0, o1, sem):
+        A.activation(T.pk[:, 16 * o0:16 * o1], win(o0, o1), copy).then_inc(sem, 1)
+
+    V.memset(T.z32[:], 0.0).then_inc(S.ms, 1)
+    V.memset(T.s32[:], 0.0).then_inc(S.ms, 1)
+    V.wait_ge(S.ldh, 16)
+    V.tensor_copy(T.hsf[:], T.hsi[:]).then_inc(S.h, 1)
+    h[0] += 1
+    V.wait_ge(S.h, 1)
+    V.wait_ge(S.ldi, 16)
+    hashes(0, 1, 1)
+    A.wait_ge(S.ldm, 16)
+    A.wait_ge(S.off_s, 1)
+    gather_a(0, L, S.gk0)
+    V.wait_ge(S.ldm, 16)
+    for i, ks in enumerate(GROUPS):
+        V.wait_ge(S["id%d" % i], len(topo.engines(core, peer[ks[0]])) * len(ks))
+        hashes(ks[0], ks[-1] + 1, i + 2)
+        A.wait_ge(S.off_s, i + 2)
+        gather_v(ks[0] * L, (ks[0] + 1) * L, S["gk%d" % ks[0]])
+        gather_a(ks[1] * L, (ks[1] + 1) * L, S["gk%d" % ks[1]])
+        if len(ks) == 3:
+            m = ks[2] * L + L // 2
+            gather_v(ks[2] * L, m, S["gk%d" % ks[2]])
+            gather_a(m, (ks[2] + 1) * L, S.g7b)
+    V.wait_ge(S.sel, 5)
+    for c in range(4):
+        V.tensor_copy(T.s0[:, c:128:4], T.z32[:]).then_inc(S.exp, 1)
+    for c in range(4):
+        V.tensor_copy(T.sf[:, c:128:4], T.s32[:]).then_inc(S.exp, 1)
+
+    def arrived(q, queue):
+        k = rank ^ q
+        if k == 0:
+            queue.wait_ge(S.gk0, 1)
+        else:
+            n = len(topo.engines(T.cores[q], core))
+            queue.wait_ge(S["pk_s%d" % q], n if k == 7 else n // 2)
+
+    def pick(q, b):
+        if q == rank:
+            return T.pk[:, b * H:(b + 1) * H]
+        return T.ld[:, q * K + b * H:q * K + (b + 1) * H]
+
+    ps, pr, vs, ts = [T.psa, T.psb], [T.pra, T.prb], [S.va, S.vb], [S.ta, S.tb]
+    P.wait_ge(S.exp, 8)
+    arrived(0, P)
+    for b in range(2):
+        P.matmul(ps[b][:, 0:H], T.s0[:], pick(0, b), True, True).then_inc(ts[b], 1)
+    for q in range(1, 8):
+        arrived(q, V)
+        for b in range(2):
+            V.wait_ge(ts[b], q)
+            V.tensor_tensor(pr[b][:], ps[b][:, 0:H], pick(q, b), AluOpType.mult).then_inc(vs[b], 1)
+            P.wait_ge(vs[b], q)
+            if q < 7:
+                P.matmul(ps[b][:, 0:H], T.sf[:], pr[b][:], True, True).then_inc(ts[b], 1)
+            else:
+                P.matmul(ps[b][0:32, 0:H], T.s32[:], pr[b][:], True, True).then_inc(ts[b], 1)
+
+    A.wait_ge(S.ta, 8)
+    A.activation(T.ysb[:, 0:H], T.psa[0:32, 0:H], copy).then_inc(S.ya, 1)
+    A.wait_ge(S.ya, 1)
+    A.dma_start(T.y[:, 0:H], T.ysb[:, 0:H]).then_inc(S.sta, 16)
+    A.wait_ge(S.sta, 16)
+    V.wait_ge(S.tb, 8)
+    V.tensor_copy(T.ysb[:, H:K], T.psb[0:32, 0:H]).then_inc(S.yb, 1)
+    g.sync.wait_ge(S.yb, 1)
+    g.sync.dma_start(T.y[:, H:K], T.ysb[:, H:K]).then_inc(S.stb, 16)
+    g.sync.wait_ge(S.stb, 16)

@@ -4,6 +4,8 @@ from concourse.mybir import AluOpType, ActivationFunctionType
 K, D = 256, 4096
 L = K // 16
 H = K // 2
+NS = 4
+W = K // NS
 GROUPS = [(1, 2), (3, 4), (5, 6, 7)]
 
 SCRATCH = {
@@ -21,14 +23,17 @@ SCRATCH = {
     "z32": ("sbuf", [128, 32], "float32"),
     "sf": ("sbuf", [128, 128], "float32"),
     "s0": ("sbuf", [128, 128], "bfloat16"),
-    "pra": ("sbuf", [128, H], "float32"),
-    "prb": ("sbuf", [128, H], "float32"),
-    "ysb": ("sbuf", [32, K], "float32"),
-    "psa": ("psum", [128, 512], "float32"),
-    "psb": ("psum", [128, 512], "float32"),
+    "pr": ("sbuf", [128, K], "float32"),
+    "yt": ("sbuf", [128, 64], "float32"),
+    "ps0": ("psum", [128, 512], "float32"),
+    "ps1": ("psum", [128, 512], "float32"),
+    "ps2": ("psum", [128, 512], "float32"),
+    "ps3": ("psum", [128, 512], "float32"),
 }
-SEMAPHORES = (["ldd", "ldi", "ldh", "ldm", "sent", "h", "off_s", "sel", "ms", "exp", "va", "vb", "ta", "tb",
+SEMAPHORES = (["ldd", "ldi", "ldh", "ldm", "sent", "h", "off_s", "sel", "ms", "expd", "o0", "o1",
                "ya", "yb", "sta", "stb", "g7b"]
+              + ["v_s%d" % b for b in range(NS)]
+              + ["t_s%d" % b for b in range(NS)]
               + ["id%d" % i for i in range(len(GROUPS))]
               + ["gk%d" % k for k in range(8)]
               + ["pk_s%d" % q for q in range(8)])
@@ -54,11 +59,14 @@ def rank_program(g, core, T, topo):
     S = T.sem
     V, P, A = g.vector, g.tensor, g.scalar
     copy = ActivationFunctionType.Copy
+    mult, add = AluOpType.mult, AluOpType.add
 
     g.sync.dma_start(T.idd[:], T.ids[:]).then_inc(S.ldd, 16)
     A.dma_start(T.idl[:, 0:L], T.ids[:]).then_inc(S.ldi, 16)
     A.dma_start(T.hsi[:], T.hs[:]).then_inc(S.ldh, 16)
-    g.sync.dma_start(T.tab[:], T.mat[:]).then_inc(S.ldm, 16)
+    g.sync.dma_start(T.tab[:, 0:D // 2], T.mat[:, 0:D // 2]).then_inc(S.ldm, 16)
+    g.sync.wait_ge(S.ldd, 16)
+    g.sync.dma_start(T.tab[:, D // 2:D], T.mat[:, D // 2:D]).then_inc(S.ldm, 16)
 
     sent = 0
     g.wait_ge(S.ldd, 16)
@@ -94,7 +102,7 @@ def rank_program(g, core, T, topo):
 
     def hashes(k0, k1, n):
         c = slice(k0 * L, k1 * L)
-        V.tensor_scalar(T.t1[:, c], T.idl[:, c], T.hsf[:, 0:1], T.hsf[:, 1:2], AluOpType.mult, AluOpType.add).then_inc(S.h, 1)
+        V.tensor_scalar(T.t1[:, c], T.idl[:, c], T.hsf[:, 0:1], T.hsf[:, 1:2], mult, add).then_inc(S.h, 1)
         h[0] += 1
         V.wait_ge(S.h, h[0])
         V.tensor_scalar(T.t2[:, c], T.t1[:, c], 2, D - 1, AluOpType.logical_shift_right, AluOpType.bitwise_and).then_inc(S.h, 1)
@@ -120,25 +128,23 @@ def rank_program(g, core, T, topo):
     V.wait_ge(S.h, 1)
     V.wait_ge(S.ldi, 16)
     hashes(0, 1, 1)
-    A.wait_ge(S.ldm, 16)
+    A.wait_ge(S.ldm, 32)
     A.wait_ge(S.off_s, 1)
     gather_a(0, L, S.gk0)
-    V.wait_ge(S.ldm, 16)
+    V.wait_ge(S.ldm, 32)
     for i, ks in enumerate(GROUPS):
         V.wait_ge(S["id%d" % i], len(topo.engines(core, peer[ks[0]])) * len(ks))
         hashes(ks[0], ks[-1] + 1, i + 2)
         A.wait_ge(S.off_s, i + 2)
         gather_v(ks[0] * L, (ks[0] + 1) * L, S["gk%d" % ks[0]])
         gather_a(ks[1] * L, (ks[1] + 1) * L, S["gk%d" % ks[1]])
-        if len(ks) == 3:
-            m = ks[2] * L + L // 2
-            gather_v(ks[2] * L, m, S["gk%d" % ks[2]])
-            gather_a(m, (ks[2] + 1) * L, S.g7b)
+    gather_v(7 * L, 7 * L + L // 2, S.gk7)
+    gather_a(7 * L + L // 2, 8 * L, S.g7b)
     V.wait_ge(S.sel, 5)
     for c in range(4):
-        V.tensor_copy(T.s0[:, c:128:4], T.z32[:]).then_inc(S.exp, 1)
+        V.tensor_copy(T.s0[:, c:128:4], T.z32[:]).then_inc(S.expd, 1)
     for c in range(4):
-        V.tensor_copy(T.sf[:, c:128:4], T.s32[:]).then_inc(S.exp, 1)
+        V.tensor_copy(T.sf[:, c:128:4], T.s32[:]).then_inc(S.expd, 1)
 
     def arrived(q, queue):
         k = rank ^ q
@@ -150,32 +156,45 @@ def rank_program(g, core, T, topo):
 
     def pick(q, b):
         if q == rank:
-            return T.pk[:, b * H:(b + 1) * H]
-        return T.ld[:, q * K + b * H:q * K + (b + 1) * H]
+            return T.pk[:, b * W:(b + 1) * W]
+        return T.ld[:, q * K + b * W:q * K + (b + 1) * W]
 
-    ps, pr, vs, ts = [T.psa, T.psb], [T.pra, T.prb], [S.va, S.vb], [S.ta, S.tb]
-    P.wait_ge(S.exp, 8)
+    ps = [T.ps0, T.ps1, T.ps2, T.ps3]
+    vs = [S["v_s%d" % b] for b in range(NS)]
+    ts = [S["t_s%d" % b] for b in range(NS)]
+    outs = [S.o0, S.o1]
+    P.wait_ge(S.expd, 8)
     arrived(0, P)
-    for b in range(2):
-        P.matmul(ps[b][:, 0:H], T.s0[:], pick(0, b), True, True).then_inc(ts[b], 1)
+    for b in range(NS):
+        P.matmul(ps[b][:, 0:W], T.s0[:], pick(0, b), True, True).then_inc(ts[b], 1)
     for q in range(1, 8):
         arrived(q, V)
-        for b in range(2):
+        for b in range(NS):
+            pr = T.pr[:, b * W:(b + 1) * W]
             V.wait_ge(ts[b], q)
-            V.tensor_tensor(pr[b][:], ps[b][:, 0:H], pick(q, b), AluOpType.mult).then_inc(vs[b], 1)
+            V.tensor_tensor(pr, ps[b][:, 0:W], pick(q, b), mult).then_inc(vs[b], 1)
             P.wait_ge(vs[b], q)
             if q < 7:
-                P.matmul(ps[b][:, 0:H], T.sf[:], pr[b][:], True, True).then_inc(ts[b], 1)
-            else:
-                P.matmul(ps[b][0:32, 0:H], T.s32[:], pr[b][:], True, True).then_inc(ts[b], 1)
+                P.matmul(ps[b][:, 0:W], T.sf[:], pr, True, True).then_inc(ts[b], 1)
+            elif b % 2:
+                P.matmul(ps[b - 1][:, 0:32], T.pr[:, (b - 1) * W:(b + 1) * W], T.s32[:], True, True).then_inc(outs[b // 2], 1)
 
-    A.wait_ge(S.ta, 8)
-    A.activation(T.ysb[:, 0:H], T.psa[0:32, 0:H], copy).then_inc(S.ya, 1)
+    for b, sem in ((0, S.ya), (1, S.yb)):
+        V.wait_ge(outs[b], 1)
+        V.transpose(T.yt[:, 32 * b:32 * (b + 1)], ps[2 * b][:, 0:32]).then_inc(sem, 1)
+
+    def store(queue, b, blocks, sem):
+        for i in blocks:
+            j = H * b + 32 * i
+            queue.dma_start(T.y[:, j:j + 32], T.yt[32 * i:32 * (i + 1), 32 * b:32 * (b + 1)]).then_inc(sem, 16)
+
     A.wait_ge(S.ya, 1)
-    A.dma_start(T.y[:, 0:H], T.ysb[:, 0:H]).then_inc(S.sta, 16)
-    A.wait_ge(S.sta, 16)
-    V.wait_ge(S.tb, 8)
-    V.tensor_copy(T.ysb[:, H:K], T.psb[0:32, 0:H]).then_inc(S.yb, 1)
+    store(A, 0, (0, 1), S.sta)
+    A.wait_ge(S.yb, 1)
+    store(A, 1, (0, 1), S.sta)
+    A.wait_ge(S.sta, 64)
+    g.sync.wait_ge(S.ya, 1)
+    store(g.sync, 0, (2, 3), S.stb)
     g.sync.wait_ge(S.yb, 1)
-    g.sync.dma_start(T.y[:, H:K], T.ysb[:, H:K]).then_inc(S.stb, 16)
-    g.sync.wait_ge(S.stb, 16)
+    store(g.sync, 1, (2, 3), S.stb)
+    g.sync.wait_ge(S.stb, 64)

from concourse.bass import DstId, RemoteDMATransfer
from concourse.mybir import AluOpType, ActivationFunctionType

K, D = 256, 4096
L = K // 16
H = K // 2
NS = 4
W = K // NS
GROUPS = [(1, 2), (3, 4), (5, 6, 7)]

SCRATCH = {
    "idd": ("dram", [128, L], "int32"),
    "idl": ("sbuf", [128, 8 * L], "int32"),
    "hsi": ("sbuf", [128, 2], "int32"),
    "hsf": ("sbuf", [128, 2], "float32"),
    "t1": ("sbuf", [128, 8 * L], "int32"),
    "t2": ("sbuf", [128, 8 * L], "int32"),
    "off": ("sbuf", [128, 8 * L], "uint16"),
    "tab": ("sbuf", [128, D], "bfloat16"),
    "pk": ("sbuf", [128, 8 * K], "bfloat16"),
    "ld": ("sbuf", [128, 8 * K], "bfloat16"),
    "s32": ("sbuf", [128, 32], "float32"),
    "z32": ("sbuf", [128, 32], "float32"),
    "sf": ("sbuf", [128, 128], "float32"),
    "s0": ("sbuf", [128, 128], "bfloat16"),
    "pr": ("sbuf", [128, K], "float32"),
    "yt": ("sbuf", [128, 64], "float32"),
    "ps0": ("psum", [128, 512], "float32"),
    "ps1": ("psum", [128, 512], "float32"),
    "ps2": ("psum", [128, 512], "float32"),
    "ps3": ("psum", [128, 512], "float32"),
}
SEMAPHORES = (["ldd", "ldi", "ldh", "ldm", "sent", "h", "off_s", "sel", "ms", "expd", "o0", "o1",
               "ya", "yb", "sta", "stb", "g7b"]
              + ["v_s%d" % b for b in range(NS)]
              + ["t_s%d" % b for b in range(NS)]
              + ["id%d" % i for i in range(len(GROUPS))]
              + ["gk%d" % k for k in range(8)]
              + ["pk_s%d" % q for q in range(8)])


def bits(engines):
    m = 0
    for e in engines:
        m |= 1 << e
    return m


def dst(topo, d, core):
    rid, pid = topo.addr(d, core)
    return DstId(rid=rid, pnc=pid)


def rank_program(g, core, T, topo):
    rank = T.rank_of(core)
    if rank is None:
        return
    peer = [T.cores[rank ^ k] for k in range(8)]
    S = T.sem
    V, P, A = g.vector, g.tensor, g.scalar
    copy = ActivationFunctionType.Copy
    mult, add = AluOpType.mult, AluOpType.add

    g.sync.dma_start(T.idd[:], T.ids[:]).then_inc(S.ldd, 16)
    A.dma_start(T.idl[:, 0:L], T.ids[:]).then_inc(S.ldi, 16)
    A.dma_start(T.hsi[:], T.hs[:]).then_inc(S.ldh, 16)
    g.sync.dma_start(T.tab[:, 0:D // 2], T.mat[:, 0:D // 2]).then_inc(S.ldm, 16)
    g.sync.wait_ge(S.ldd, 16)
    g.sync.dma_start(T.tab[:, D // 2:D], T.mat[:, D // 2:D]).then_inc(S.ldm, 16)

    sent = 0
    g.wait_ge(S.ldd, 16)
    for i, ks in enumerate(GROUPS):
        eng = topo.engines(core, peer[ks[0]])
        g.remote_dma_fused([RemoteDMATransfer(
            dst_ids=[dst(topo, peer[k], core) for k in ks], dma_engine_mask=bits(eng), remote_sem=S["id%d" % i],
            srcs=[T.idd[:]], dsts=[T.idl[:, k * L:(k + 1) * L] for k in ks])], local_sem=S.sent)
        sent += len(eng)
    g.wait_ge(S.ms, 2)
    g.affine_select(T.z32[:], T.z32[:], [[-16, 8], [-1, 4]], AluOpType.not_equal, 1.0, 0, 1).then_inc(S.sel, 1)
    for a in range(4):
        g.affine_select(T.s32[:], T.s32[:], [[-16, 8], [-1, 4]], AluOpType.not_equal, 1.0, -4 * a, 1).then_inc(S.sel, 1)
        g.wait_ge(S.sel, a + 2)
    for ks in [(1, 2), (3, 4), (5, 6), (7,)]:
        for k in ks:
            g.wait_ge(S["gk%d" % k], 1)
            if k == 7:
                g.wait_ge(S.g7b, 1)
        tr = []
        for i, k in enumerate(ks):
            eng = topo.engines(core, peer[k])
            n = len(eng) // len(ks)
            eng = eng[i * n:(i + 1) * n]
            tr.append(RemoteDMATransfer(
                dst_ids=[dst(topo, peer[k], core)], dma_engine_mask=bits(eng), remote_sem=S["pk_s%d" % rank],
                srcs=[T.pk[:, k * K:(k + 1) * K]], dsts=[T.ld[:, rank * K:(rank + 1) * K]]))
            sent += n
        g.remote_dma_fused(tr, local_sem=S.sent)
    g.wait_ge(S.sent, sent)

    h = [0]

    def hashes(k0, k1, n):
        c = slice(k0 * L, k1 * L)
        V.tensor_scalar(T.t1[:, c], T.idl[:, c], T.hsf[:, 0:1], T.hsf[:, 1:2], mult, add).then_inc(S.h, 1)
        h[0] += 1
        V.wait_ge(S.h, h[0])
        V.tensor_scalar(T.t2[:, c], T.t1[:, c], 2, D - 1, AluOpType.logical_shift_right, AluOpType.bitwise_and).then_inc(S.h, 1)
        h[0] += 1
        V.wait_ge(S.h, h[0])
        V.tensor_copy(T.off[:, c], T.t2[:, c]).then_inc(S.off_s, 1)
        V.wait_ge(S.off_s, n)

    def win(o0, o1):
        return T.tab[:, 0:D].indirect(T.off[:, o0:o1])

    def gather_v(o0, o1, sem):
        V.tensor_copy(T.pk[:, 16 * o0:16 * o1], win(o0, o1)).then_inc(sem, 1)

    def gather_a(o0, o1, sem):
        A.activation(T.pk[:, 16 * o0:16 * o1], win(o0, o1), copy).then_inc(sem, 1)

    V.memset(T.z32[:], 0.0).then_inc(S.ms, 1)
    V.memset(T.s32[:], 0.0).then_inc(S.ms, 1)
    V.wait_ge(S.ldh, 16)
    V.tensor_copy(T.hsf[:], T.hsi[:]).then_inc(S.h, 1)
    h[0] += 1
    V.wait_ge(S.h, 1)
    V.wait_ge(S.ldi, 16)
    hashes(0, 1, 1)
    A.wait_ge(S.ldm, 32)
    A.wait_ge(S.off_s, 1)
    gather_a(0, L, S.gk0)
    V.wait_ge(S.ldm, 32)
    for i, ks in enumerate(GROUPS):
        V.wait_ge(S["id%d" % i], len(topo.engines(core, peer[ks[0]])) * len(ks))
        hashes(ks[0], ks[-1] + 1, i + 2)
        A.wait_ge(S.off_s, i + 2)
        gather_v(ks[0] * L, (ks[0] + 1) * L, S["gk%d" % ks[0]])
        gather_a(ks[1] * L, (ks[1] + 1) * L, S["gk%d" % ks[1]])
    gather_v(7 * L, 7 * L + L // 2, S.gk7)
    gather_a(7 * L + L // 2, 8 * L, S.g7b)
    V.wait_ge(S.sel, 5)
    for c in range(4):
        V.tensor_copy(T.s0[:, c:128:4], T.z32[:]).then_inc(S.expd, 1)
    for c in range(4):
        V.tensor_copy(T.sf[:, c:128:4], T.s32[:]).then_inc(S.expd, 1)

    def arrived(q, queue):
        k = rank ^ q
        if k == 0:
            queue.wait_ge(S.gk0, 1)
        else:
            n = len(topo.engines(T.cores[q], core))
            queue.wait_ge(S["pk_s%d" % q], n if k == 7 else n // 2)

    def pick(q, b):
        if q == rank:
            return T.pk[:, b * W:(b + 1) * W]
        return T.ld[:, q * K + b * W:q * K + (b + 1) * W]

    ps = [T.ps0, T.ps1, T.ps2, T.ps3]
    vs = [S["v_s%d" % b] for b in range(NS)]
    ts = [S["t_s%d" % b] for b in range(NS)]
    outs = [S.o0, S.o1]
    P.wait_ge(S.expd, 8)
    arrived(0, P)
    for b in range(NS):
        P.matmul(ps[b][:, 0:W], T.s0[:], pick(0, b), True, True).then_inc(ts[b], 1)
    for q in range(1, 8):
        arrived(q, V)
        for b in range(NS):
            pr = T.pr[:, b * W:(b + 1) * W]
            V.wait_ge(ts[b], q)
            V.tensor_tensor(pr, ps[b][:, 0:W], pick(q, b), mult).then_inc(vs[b], 1)
            P.wait_ge(vs[b], q)
            if q < 7:
                P.matmul(ps[b][:, 0:W], T.sf[:], pr, True, True).then_inc(ts[b], 1)
            elif b % 2:
                P.matmul(ps[b - 1][:, 0:32], T.pr[:, (b - 1) * W:(b + 1) * W], T.s32[:], True, True).then_inc(outs[b // 2], 1)

    for b, sem in ((0, S.ya), (1, S.yb)):
        V.wait_ge(outs[b], 1)
        V.transpose(T.yt[:, 32 * b:32 * (b + 1)], ps[2 * b][:, 0:32]).then_inc(sem, 1)

    def store(queue, b, blocks, sem):
        for i in blocks:
            j = H * b + 32 * i
            queue.dma_start(T.y[:, j:j + 32], T.yt[32 * i:32 * (i + 1), 32 * b:32 * (b + 1)]).then_inc(sem, 16)

    A.wait_ge(S.ya, 1)
    store(A, 0, (0, 1), S.sta)
    A.wait_ge(S.yb, 1)
    store(A, 1, (0, 1), S.sta)
    A.wait_ge(S.sta, 64)
    g.sync.wait_ge(S.ya, 1)
    store(g.sync, 0, (2, 3), S.stb)
    g.sync.wait_ge(S.yb, 1)
    store(g.sync, 1, (2, 3), S.stb)
    g.sync.wait_ge(S.stb, 64)
